import numpy as np
import ml_dtypes


def mxq(x, axis, fmt="e4m3"):
    dtype, down = {"e4m3": (ml_dtypes.float8_e4m3fn, 7), "e5m2": (ml_dtypes.float8_e5m2, 14)}[fmt]
    v = np.moveaxis(np.asarray(x, np.float32).astype(ml_dtypes.bfloat16).astype(np.float64), axis, -1)
    blocks = v.reshape(v.shape[:-1] + (-1, 32))
    amax = np.abs(blocks).max(-1, keepdims=True)
    byte = np.maximum(np.where(amax > 0, np.frexp(amax)[1] - 1 + 127, 0) - down, 1)
    scale = np.exp2(byte - 127.0)
    codes = (blocks / scale).astype(np.float32).astype(dtype).astype(np.float64)
    return np.moveaxis((codes * scale).reshape(v.shape), -1, axis)


WIDE = False


def mx_kscale(k):
    if not WIDE:
        return np.ones(k)
    levels = np.array([10, -10, 5, -5, 0])
    if k % 512:
        return np.exp2(np.random.permutation(np.resize(levels, k // 32))).repeat(32)
    a = np.empty((k // 512, 16))
    for p in range(k // 512):
        a[p, :8] = np.random.permutation(np.resize(levels, 8))
        for g in range(8):
            far = levels[np.abs(levels - a[p, g]) >= 10]
            a[p, g + 8] = far[np.random.randint(len(far))]
    return np.exp2(a.ravel()).repeat(32)


def f64(x):
    return np.asarray(x).astype(np.float64)


def striped(idx):
    return np.tile(idx.reshape(-1, 16).T, (8, 1)).astype(np.uint16)


def unstriped(offs):
    return offs[:16].T.reshape(-1).astype(np.int64)


def pack_weight(w):
    k, n = w.shape
    w = f64(np.asarray(w, np.float32).astype(ml_dtypes.bfloat16)).reshape(k // 32, 32, n)
    amax = np.abs(w).max(1)
    byte = np.clip(np.where(amax > 0, np.frexp(amax)[1] - 1 + 127 - 7, 1), 1, 254)
    scaled = (w * np.exp2(127.0 - byte)[:, None, :]).reshape(k, n).astype(np.float32)
    words = np.ascontiguousarray(scaled.reshape(k // 512, 128, 4, n).transpose(0, 1, 3, 2)).astype(ml_dtypes.float8_e4m3fn).view(np.uint8)
    return words, np.ascontiguousarray(byte.astype(np.uint8).reshape(k // 512, 16, n))


def unpack_weight(words, scales):
    g, p, n, _ = words.shape
    vals = np.ascontiguousarray(words).view(ml_dtypes.float8_e4m3fn).astype(np.float64) * np.repeat(np.exp2(scales.astype(np.float64) - 127.0), 8, axis=1)[..., None]
    return vals.transpose(0, 1, 3, 2).reshape(g * 512, n)


def sigmoid(v):
    return 1.0 / (1.0 + np.exp(-np.maximum(v, -700.0)))


K, T, S, V, U, D = 1024, 2048, 512, 512, 1024, 8


def setup_inputs():
    n = np.random.standard_normal
    s = mx_kscale(K)[:, None]
    packed_xT = pack_weight(n((K, T)) * s)
    return {
        "x_words": packed_xT[0],
        "x_scales": packed_xT[1],
        "hT": (n((K, V)) / np.sqrt(K) / s).astype(np.float32),
        "offs": striped(np.random.permutation(T)[:S]),
        "code": striped(np.random.permutation(np.concatenate([np.arange(S), np.random.randint(0, S, U - S)]))),
    }


def reference(x_words, x_scales, hT, offs, code):
    hTq = mxq(f64(hT), 0, "e4m3")
    xq = unpack_weight(x_words, x_scales)[:, unstriped(offs)]
    y = hTq.T @ xq
    top = y.max(axis=1, keepdims=True)
    p = y * (sigmoid(6.0 * (y - (0.4 * top))))
    gg = p[:, unstriped(code)]
    return gg.reshape(len(gg), -1, D).max(axis=2)

@@ -1,0 +1,215 @@
+from contextlib import ExitStack
+
+import concourse.mybir as mybir
+
+K, T, S, V, U, D = 1024, 2048, 512, 512, 1024, 8
+FLOPS = 2 * K * V * S
+
+F32 = mybir.dt.float32
+BF16 = mybir.dt.bfloat16
+I32 = mybir.dt.int32
+U32 = mybir.dt.uint32
+U16 = mybir.dt.uint16
+U8 = mybir.dt.uint8
+FP8X4 = mybir.dt.float8_e4m3fn_x4
+ALU = mybir.AluOpType
+ACT = mybir.ActivationFunctionType
+AXIS = mybir.AxisListType
+
+P = 128
+PACK = 4
+K_PASS = P * PACK
+PASSES = K // K_PASS
+TILES = V // P
+RUN = 4
+
+
+def tile_picked_yplaid_max_p_kernel(tc, x_words, x_scales, hT, offs, code, out):
+    nc = tc.nc
+    with ExitStack() as ctx:
+        keep = ctx.enter_context(tc.tile_pool(name="keep", bufs=1))
+        ring = ctx.enter_context(tc.tile_pool(name="ring", bufs=2))
+        psum = ctx.enter_context(tc.psum_pool(name="psum", bufs=1))
+
+        offs_sb = keep.tile([P, S // 16], U16, name="offs_sb")
+        code_sb = keep.tile([P, U // 16], U16, name="code_sb")
+        table = [keep.tile([P, T], U32, name="table%d" % o, align_bytes=64) for o in range(PASSES)]
+        table_scales = keep.tile([P, T], U8, name="table_scales", align_bytes=64)
+        picked = [keep.tile([P, S], U32, name="picked%d" % o, align_bytes=64) for o in range(PASSES)]
+        picked_scales = keep.tile([P, S], U8, name="picked_scales", align_bytes=64)
+        planes = keep.tile([P, 11 * S], F32, name="planes", align_bytes=64)
+        p_at = [0, 4, 3, 7]
+        s_at = [1, 5, 10, 8]
+        y_at = [9, 2, 6, 5]
+
+        def plane(at, first=0, last=S):
+            return planes[:, at * S + first : at * S + last]
+
+        groups = [(0, P), (P, P), (2 * P, 2 * P)]
+        raw = {}
+        grouped = {}
+        h_codes = {}
+        h_scales = {}
+        for g, (c0, w) in enumerate(groups):
+            for o in range(PASSES):
+                raw[g, o] = keep.tile([P, PACK, w], F32, name="raw%d_%d" % (g, o))
+            grouped[g] = keep.tile([P, PASSES * w * PACK], BF16, name="grouped%d" % g, align_bytes=64)
+            h_codes[g] = keep.tile([P, PASSES * w], U32, name="h_codes%d" % g, align_bytes=64)
+            h_scales[g] = keep.tile([P, PASSES * w], U8, name="h_scales%d" % g, align_bytes=64)
+
+        def load_table(o):
+            nc.sync.dma_start(
+                out=table[o][:].bitcast(I32),
+                in_=x_words[o].rearrange("p n r -> p (n r)").bitcast(I32),
+            )
+
+        def load_h(g, o):
+            c0, w = groups[g]
+            rows = hT[o * K_PASS : (o + 1) * K_PASS, c0 : c0 + w]
+            nc.sync.dma_start(out=raw[g, o][:], in_=rows.rearrange("(p j) t -> p j t", j=PACK))
+
+        def interleave(copy, g, o):
+            w = groups[g][1]
+            dst = grouped[g][:, o * w * PACK : (o + 1) * w * PACK]
+            copy(
+                out=dst.rearrange("p (c i j) -> p c j i", i=RUN, j=PACK),
+                in_=raw[g, o][:].rearrange("p j (c i) -> p c j i", i=RUN),
+            )
+
+        def quantize(g, o0, o1):
+            w = groups[g][1]
+            nc.vector.quantize_mx(
+                out=h_codes[g][:, o0 * w : o1 * w].bitcast(FP8X4),
+                scales=h_scales[g][:, o0 * w : o1 * w],
+                in_=grouped[g][:, o0 * w * PACK : o1 * w * PACK],
+            )
+
+        HALF = S // 2
+        pieces = [[(0, HALF), (HALF, S)]] + [[(0, S)]] * (TILES - 1)
+        banks = {}
+        for t in range(TILES):
+            for first, last in pieces[t]:
+                banks[t, first] = psum.tile([P, last - first], F32, name="bank%d_%d" % (t, first))
+
+        def pick(o, first, last):
+            nc.vector.tensor_copy(picked[o][:, first:last], table[o][:].indirect(offs_sb[:, first // 16 : last // 16]))
+
+        def product(t, o, first, last):
+            g = min(t, 2)
+            c0, w = groups[g]
+            col = o * w + t * P - c0
+            nc.tensor.matmul_mx(
+                out=banks[t, first][:],
+                lhsT=h_codes[g][:, col : col + P].bitcast(FP8X4),
+                lhsT_scale=h_scales[g][:, col : col + P],
+                rhs=picked[o][:, first:last].bitcast(FP8X4),
+                rhs_scale=picked_scales[4 * o : P, first:last],
+                start=(o == 0),
+                stop=(o == PASSES - 1),
+            )
+
+        def fade_first():
+            bias = None
+            for first, last in pieces[0]:
+                so_far = bias
+                if so_far is None:
+                    bias = keep.tile([P, 1], F32, name="bias_half")[:]
+                else:
+                    bias = grouped[2][:, 0:2].bitcast(F32)
+                nc.vector.tensor_scalar(
+                    out=plane(y_at[0], first, last), in0=banks[0, first][:], scalar1=-2.4, scalar2=so_far,
+                    op0=ALU.mult, op1=ALU.min, accum_out=bias,
+                )
+            for first, last in pieces[0]:
+                nc.scalar.activation(
+                    out=plane(s_at[0], first, last), in_=plane(y_at[0], first, last),
+                    func=ACT.Sigmoid, bias=bias, scale=-2.5,
+                )
+
+        def weigh_first():
+            for first, last in pieces[0]:
+                nc.vector.tensor_tensor(
+                    out=plane(p_at[0], first, last), in0=banks[0, first][:], in1=plane(s_at[0], first, last), op=ALU.mult
+                )
+
+        def fade(t):
+            top = keep.tile([P, 1], F32, name="top%d" % t)
+            nc.vector.tensor_scalar(
+                out=plane(y_at[t]), in0=banks[t, 0][:], scalar1=1.0, scalar2=None,
+                op0=ALU.mult, op1=ALU.max, accum_out=top[:],
+            )
+            bias = keep.tile([P, 1], F32, name="bias%d" % t)
+            nc.scalar.mul(bias[:], top[:], -2.4)
+            nc.scalar.activation(out=plane(s_at[t]), in_=plane(y_at[t]), func=ACT.Sigmoid, bias=bias[:], scale=6.0)
+
+        def weigh(engine, t):
+            engine.tensor_tensor(out=plane(p_at[t]), in0=plane(y_at[t]), in1=plane(s_at[t]), op=ALU.mult)
+
+        def fetch(t):
+            fetched = ring.tile([P, U], F32, name="fetched")
+            window = planes[:, p_at[t] * S : (p_at[t] + 3) * S]
+            nc.vector.tensor_copy(fetched[:], window.indirect(code_sb[:]))
+            return fetched
+
+        def best(t, fetched):
+            if t == 0:
+                result = grouped[2][:, 0 : 2 * U // D].bitcast(F32)
+            else:
+                result = keep.tile([P, U // D], F32, name="result%d" % t)[:]
+            nc.vector.tensor_reduce(
+                out=result, in_=fetched[:].rearrange("p (v d) -> p v d", d=D), axis=AXIS.X, op=ALU.max
+            )
+            nc.sync.dma_start(out=out[t * P : (t + 1) * P, :], in_=result)
+
+        warm = keep.tile([P, 2], F32, name="warm")
+        nc.vector.memset(warm[:, 0:1], 0.0)
+        nc.scalar.activation(out=warm[:, 1:2], in_=warm[:, 0:1], func=ACT.Sigmoid)
+        nc.gpsimd.memset(table_scales[:].bitcast(I32), 0)
+        for q in range(4):
+            nc.sync.dma_start(
+                out=table_scales[32 * q : 32 * q + 4 * PASSES, :].bitcast(I32),
+                in_=x_scales[:, 4 * q : 4 * q + 4, :].bitcast(I32),
+            )
+        nc.sync.dma_start(offs_sb[:], offs)
+        load_table(0)
+        load_h(0, 0)
+        load_h(0, 1)
+        load_table(1)
+        load_h(1, 0)
+        load_h(1, 1)
+        load_h(2, 0)
+        nc.sync.dma_start(code_sb[:], code)
+        load_h(2, 1)
+
+        nc.vector.tensor_copy(picked_scales[:], table_scales[:].indirect(offs_sb[:]))
+        pick(0, 0, S)
+        interleave(nc.scalar.copy, 0, 0)
+        interleave(nc.scalar.copy, 0, 1)
+        quantize(0, 0, 2)
+        for first, last in pieces[0]:
+            product(0, 0, first, last)
+        for first, last in pieces[0]:
+            pick(1, first, last)
+            product(0, 1, first, last)
+        interleave(nc.scalar.copy, 1, 0)
+        interleave(nc.scalar.copy, 1, 1)
+        fade_first()
+        quantize(1, 0, 2)
+        product(1, 0, 0, S)
+        product(1, 1, 0, S)
+        weigh_first()
+        interleave(nc.scalar.copy, 2, 0)
+        interleave(nc.scalar.copy, 2, 1)
+        fade(1)
+        fetched = fetch(0)
+        quantize(2, 0, 2)
+        for t in range(2, TILES):
+            product(t, 0, 0, S)
+            product(t, 1, 0, S)
+        for t in range(1, TILES):
+            best(t - 1, fetched)
+            weigh(nc.gpsimd, t)
+            if t + 1 < TILES:
+                fade(t + 1)
+            fetched = fetch(t)
+        best(TILES - 1, fetched)

@@ -21,7 +21,17 @@ PACK = 4
 K_PASS = P * PACK
 PASSES = K // K_PASS
 TILES = V // P
-RUN = 4
+RUN = 2
+SCALE_ROWS = 4
+SLOPE = 6.0
+FADE = 2.4
+GROUPS = [(0, P), (P, P), (2 * P, 2 * P)]
+HALVES = [(0, S // 2), (S // 2, S)]
+WHOLE = [(0, S)]
+P_AT = [0, 4, 3, 7]
+S_AT = [1, 5, 10, 8]
+Y_AT = [9, 2, 6, 5]
+CUTS = [0, 64, 96, U // D]
 
 
 def tile_picked_yplaid_max_p_kernel(tc, x_words, x_scales, hT, offs, code, out):
@@ -34,28 +44,24 @@ def tile_picked_yplaid_max_p_kernel(tc, x_words, x_scales, hT, offs, code, out):
         offs_sb = keep.tile([P, S // 16], U16, name="offs_sb")
         code_sb = keep.tile([P, U // 16], U16, name="code_sb")
         table = [keep.tile([P, T], U32, name="table%d" % o, align_bytes=64) for o in range(PASSES)]
-        table_scales = keep.tile([P, T], U8, name="table_scales", align_bytes=64)
-        picked = [keep.tile([P, S], U32, name="picked%d" % o, align_bytes=64) for o in range(PASSES)]
+        table_scales = keep.tile([P, T], U8, name="table_scales", tag="scales_then_words", align_bytes=64)
         picked_scales = keep.tile([P, S], U8, name="picked_scales", align_bytes=64)
+        picked = {}
         planes = keep.tile([P, 11 * S], F32, name="planes", align_bytes=64)
-        p_at = [0, 4, 3, 7]
-        s_at = [1, 5, 10, 8]
-        y_at = [9, 2, 6, 5]
+        raw, rounded, h_codes, h_scales, banks = {}, {}, {}, {}, {}
+        pieces = [HALVES] + [WHOLE] * (TILES - 1)
+        for t in range(TILES - 1):
+            for first, last in pieces[t]:
+                banks[t, first] = psum.tile([P, last - first], F32, name="bank%d_%d" % (t, first), tag="bank%d_%d" % (t, first))
 
-        def plane(at, first=0, last=S):
-            return planes[:, at * S + first : at * S + last]
+        def p_of(t):
+            return planes[:, P_AT[t] * S : (P_AT[t] + 1) * S]
 
-        groups = [(0, P), (P, P), (2 * P, 2 * P)]
-        raw = {}
-        grouped = {}
-        h_codes = {}
-        h_scales = {}
-        for g, (c0, w) in enumerate(groups):
-            for o in range(PASSES):
-                raw[g, o] = keep.tile([P, PACK, w], F32, name="raw%d_%d" % (g, o))
-            grouped[g] = keep.tile([P, PASSES * w * PACK], BF16, name="grouped%d" % g, align_bytes=64)
-            h_codes[g] = keep.tile([P, PASSES * w], U32, name="h_codes%d" % g, align_bytes=64)
-            h_scales[g] = keep.tile([P, PASSES * w], U8, name="h_scales%d" % g, align_bytes=64)
+        def s_of(t):
+            return planes[:, S_AT[t] * S : (S_AT[t] + 1) * S]
+
+        def y_of(t):
+            return planes[:, Y_AT[t] * S : (Y_AT[t] + 1) * S]
 
         def load_table(o):
             nc.sync.dma_start(
@@ -64,111 +70,93 @@ def tile_picked_yplaid_max_p_kernel(tc, x_words, x_scales, hT, offs, code, out):
             )
 
         def load_h(g, o):
-            c0, w = groups[g]
-            rows = hT[o * K_PASS : (o + 1) * K_PASS, c0 : c0 + w]
-            nc.sync.dma_start(out=raw[g, o][:], in_=rows.rearrange("(p j) t -> p j t", j=PACK))
+            c0, w = GROUPS[g]
+            raw[g, o] = keep.tile([P, PACK, w], F32, name="raw%d_%d" % (g, o))
+            k_rows = hT[o * K_PASS : (o + 1) * K_PASS, c0 : c0 + w]
+            nc.sync.dma_start(out=raw[g, o][:], in_=k_rows.rearrange("(p j) t -> p j t", j=PACK))
 
-        def interleave(copy, g, o):
-            w = groups[g][1]
-            dst = grouped[g][:, o * w * PACK : (o + 1) * w * PACK]
+        def interleave(copy, g, o, dst):
             copy(
                 out=dst.rearrange("p (c i j) -> p c j i", i=RUN, j=PACK),
                 in_=raw[g, o][:].rearrange("p j (c i) -> p c j i", i=RUN),
             )
 
-        def quantize(g, o0, o1):
-            w = groups[g][1]
+        def quantize(g, first, src):
+            words = src.shape[1] // PACK
             nc.vector.quantize_mx(
-                out=h_codes[g][:, o0 * w : o1 * w].bitcast(FP8X4),
-                scales=h_scales[g][:, o0 * w : o1 * w],
-                in_=grouped[g][:, o0 * w * PACK : o1 * w * PACK],
+                out=h_codes[g][:, first : first + words].bitcast(FP8X4),
+                scales=h_scales[g][:, first : first + words],
+                in_=src,
             )
 
-        HALF = S // 2
-        pieces = [[(0, HALF), (HALF, S)]] + [[(0, S)]] * (TILES - 1)
-        banks = {}
-        for t in range(TILES):
-            for first, last in pieces[t]:
-                banks[t, first] = psum.tile([P, last - first], F32, name="bank%d_%d" % (t, first))
-
         def pick(o, first, last):
-            nc.vector.tensor_copy(picked[o][:, first:last], table[o][:].indirect(offs_sb[:, first // 16 : last // 16]))
+            entries = offs_sb[:, first // 16 : last // 16]
+            nc.vector.tensor_copy(picked[o][:, first:last], table[o][:].indirect(entries))
 
         def product(t, o, first, last):
-            g = min(t, 2)
-            c0, w = groups[g]
+            g = min(t, len(GROUPS) - 1)
+            c0, w = GROUPS[g]
             col = o * w + t * P - c0
             nc.tensor.matmul_mx(
                 out=banks[t, first][:],
                 lhsT=h_codes[g][:, col : col + P].bitcast(FP8X4),
                 lhsT_scale=h_scales[g][:, col : col + P],
                 rhs=picked[o][:, first:last].bitcast(FP8X4),
-                rhs_scale=picked_scales[4 * o : P, first:last],
+                rhs_scale=picked_scales[SCALE_ROWS * o : P, first:last],
                 start=(o == 0),
                 stop=(o == PASSES - 1),
             )
 
-        def fade_first():
-            bias = None
-            for first, last in pieces[0]:
-                so_far = bias
-                if so_far is None:
-                    bias = keep.tile([P, 1], F32, name="bias_half")[:]
-                else:
-                    bias = grouped[2][:, 0:2].bitcast(F32)
+        def fade_scaled(t, biases):
+            so_far = None
+            for (first, last), bias in zip(pieces[t], biases):
                 nc.vector.tensor_scalar(
-                    out=plane(y_at[0], first, last), in0=banks[0, first][:], scalar1=-2.4, scalar2=so_far,
+                    out=y_of(t)[:, first:last], in0=banks[t, first][:], scalar1=-FADE, scalar2=so_far,
                     op0=ALU.mult, op1=ALU.min, accum_out=bias,
                 )
-            for first, last in pieces[0]:
+                so_far = bias
+            for first, last in pieces[t]:
                 nc.scalar.activation(
-                    out=plane(s_at[0], first, last), in_=plane(y_at[0], first, last),
-                    func=ACT.Sigmoid, bias=bias, scale=-2.5,
+                    out=s_of(t)[:, first:last], in_=y_of(t)[:, first:last],
+                    func=ACT.Sigmoid, bias=so_far, scale=-SLOPE / FADE,
                 )
 
-        def weigh_first():
-            for first, last in pieces[0]:
+        def weigh_on_vector(t):
+            for first, last in pieces[t]:
                 nc.vector.tensor_tensor(
-                    out=plane(p_at[0], first, last), in0=banks[0, first][:], in1=plane(s_at[0], first, last), op=ALU.mult
+                    out=p_of(t)[:, first:last], in0=banks[t, first][:], in1=s_of(t)[:, first:last], op=ALU.mult
                 )
 
-        def fade(t):
+        def fade_plain(t, bias):
             top = keep.tile([P, 1], F32, name="top%d" % t)
             nc.vector.tensor_scalar(
-                out=plane(y_at[t]), in0=banks[t, 0][:], scalar1=1.0, scalar2=None,
+                out=y_of(t), in0=banks[t, 0][:], scalar1=1.0, scalar2=None,
                 op0=ALU.mult, op1=ALU.max, accum_out=top[:],
             )
-            bias = keep.tile([P, 1], F32, name="bias%d" % t)
-            nc.scalar.mul(bias[:], top[:], -2.4)
-            nc.scalar.activation(out=plane(s_at[t]), in_=plane(y_at[t]), func=ACT.Sigmoid, bias=bias[:], scale=6.0)
+            nc.scalar.mul(bias[:], top[:], -FADE)
+            nc.scalar.activation(out=s_of(t), in_=y_of(t), func=ACT.Sigmoid, bias=bias[:], scale=SLOPE)
 
-        def weigh(engine, t):
-            engine.tensor_tensor(out=plane(p_at[t]), in0=plane(y_at[t]), in1=plane(s_at[t]), op=ALU.mult)
+        def weigh_on_gpsimd(t):
+            nc.gpsimd.tensor_tensor(out=p_of(t), in0=y_of(t), in1=s_of(t), op=ALU.mult)
 
         def fetch(t):
-            fetched = ring.tile([P, U], F32, name="fetched")
-            window = planes[:, p_at[t] * S : (p_at[t] + 3) * S]
-            nc.vector.tensor_copy(fetched[:], window.indirect(code_sb[:]))
+            fetched = ring.tile([P, U // D, D], F32, name="fetched")
+            window = planes[:, P_AT[t] * S : (P_AT[t] + 3) * S]
+            nc.vector.tensor_copy(fetched[:].rearrange("p v d -> p (v d)"), window.indirect(code_sb[:]))
             return fetched
 
-        def best(t, fetched):
-            if t == 0:
-                result = grouped[2][:, 0 : 2 * U // D].bitcast(F32)
-            else:
-                result = keep.tile([P, U // D], F32, name="result%d" % t)[:]
-            nc.vector.tensor_reduce(
-                out=result, in_=fetched[:].rearrange("p (v d) -> p v d", d=D), axis=AXIS.X, op=ALU.max
-            )
+        def best(fetched, result, first=0, last=U // D):
+            nc.vector.tensor_reduce(out=result[:, first:last], in_=fetched[:, first:last, :], axis=AXIS.X, op=ALU.max)
+
+        def store(t, result):
             nc.sync.dma_start(out=out[t * P : (t + 1) * P, :], in_=result)
 
-        warm = keep.tile([P, 2], F32, name="warm")
-        nc.vector.memset(warm[:, 0:1], 0.0)
-        nc.scalar.activation(out=warm[:, 1:2], in_=warm[:, 0:1], func=ACT.Sigmoid)
+
         nc.gpsimd.memset(table_scales[:].bitcast(I32), 0)
         for q in range(4):
             nc.sync.dma_start(
-                out=table_scales[32 * q : 32 * q + 4 * PASSES, :].bitcast(I32),
-                in_=x_scales[:, 4 * q : 4 * q + 4, :].bitcast(I32),
+                out=table_scales[32 * q : 32 * q + SCALE_ROWS * PASSES, :].bitcast(I32),
+                in_=x_scales[:, SCALE_ROWS * q : SCALE_ROWS * (q + 1), :].bitcast(I32),
             )
         nc.sync.dma_start(offs_sb[:], offs)
         load_table(0)
@@ -181,35 +169,63 @@ def tile_picked_yplaid_max_p_kernel(tc, x_words, x_scales, hT, offs, code, out):
         nc.sync.dma_start(code_sb[:], code)
         load_h(2, 1)
 
-        nc.vector.tensor_copy(picked_scales[:], table_scales[:].indirect(offs_sb[:]))
+        for g, (c0, w) in enumerate(GROUPS):
+            h_scales[g] = keep.tile([P, PASSES * w], U8, name="h_scales%d" % g, align_bytes=64)
+        for g in range(2):
+            rounded[g] = keep.tile([P, PASSES, P * PACK], BF16, name="rounded%d" % g, align_bytes=64)
+
+        picked[0] = keep.tile([P, S], U32, name="picked0", align_bytes=64)
         pick(0, 0, S)
-        interleave(nc.scalar.copy, 0, 0)
-        interleave(nc.scalar.copy, 0, 1)
-        quantize(0, 0, 2)
-        for first, last in pieces[0]:
+        nc.vector.tensor_copy(picked_scales[:], table_scales[:].indirect(offs_sb[:]))
+        for o in range(PASSES):
+            interleave(nc.vector.tensor_copy, 0, o, rounded[0][:, o, :])
+        h_codes[0] = keep.tile([P, PASSES * P], U32, name="h_codes0", align_bytes=64)
+        quantize(0, 0, rounded[0][:].rearrange("p o c -> p (o c)"))
+        for first, last in HALVES:
             product(0, 0, first, last)
-        for first, last in pieces[0]:
+        picked[1] = keep.tile([P, S], U32, name="picked1", tag="scales_then_words", align_bytes=64)
+        for first, last in HALVES:
             pick(1, first, last)
             product(0, 1, first, last)
-        interleave(nc.scalar.copy, 1, 0)
-        interleave(nc.scalar.copy, 1, 1)
-        fade_first()
-        quantize(1, 0, 2)
+        half_bias = keep.tile([P, 1], F32, name="half_bias")
+        biases = [keep.tile([P, 1], F32, name="bias%d" % t, tag="bias%d" % t, align_bytes=64) for t in range(TILES)]
+        h_codes[1] = keep.tile([P, PASSES * P], U32, name="h_codes1", align_bytes=64)
+        interleave(nc.vector.tensor_copy, 1, 0, rounded[1][:, 0, :])
+        fade_scaled(0, [half_bias[:], biases[0][:]])
+        quantize(1, 0, rounded[1][:, 0, :])
         product(1, 0, 0, S)
+        interleave(nc.vector.tensor_copy, 1, 1, rounded[1][:, 1, :])
+        quantize(1, P, rounded[1][:, 1, :])
         product(1, 1, 0, S)
-        weigh_first()
-        interleave(nc.scalar.copy, 2, 0)
-        interleave(nc.scalar.copy, 2, 1)
-        fade(1)
-        fetched = fetch(0)
-        quantize(2, 0, 2)
-        for t in range(2, TILES):
-            product(t, 0, 0, S)
-            product(t, 1, 0, S)
+        weigh_on_vector(0)
+        fade_plain(1, biases[1])
+        weigh_on_gpsimd(1)
+
+        wide = GROUPS[2][1]
+        late = [keep.tile([P, wide * PACK], BF16, name="late%d" % o, tag="bias%d" % o, align_bytes=64) for o in range(PASSES)]
+        for o in range(PASSES):
+            interleave(nc.scalar.copy, 2, o, late[o][:])
+        h_codes[2] = keep.tile([P, PASSES * wide], U32, name="h_codes2", align_bytes=64)
+        quantize(2, 0, late[0][:])
+        fetched = {0: fetch(0)}
+        quantize(2, wide, late[1][:])
+        for o in range(PASSES):
+            product(2, o, 0, S)
+        results = [raw[2, 1][:, t, 0 : U // D] for t in range(TILES)]
         for t in range(1, TILES):
-            best(t - 1, fetched)
-            weigh(nc.gpsimd, t)
             if t + 1 < TILES:
-                fade(t + 1)
-            fetched = fetch(t)
-        best(TILES - 1, fetched)
+                best(fetched[t - 1], results[t - 1], CUTS[0], CUTS[1])
+                fade_plain(t + 1, biases[t + 1])
+                weigh_on_gpsimd(t + 1)
+                best(fetched[t - 1], results[t - 1], CUTS[1], CUTS[2])
+            else:
+                best(fetched[t - 1], results[t - 1], CUTS[0], CUTS[2])
+            if t + 2 < TILES:
+                banks[t + 2, 0] = psum.tile([P, S], F32, name="bank3_0", tag="bank2_0")
+                for o in range(PASSES):
+                    product(t + 2, o, 0, S)
+            fetched[t] = fetch(t)
+            best(fetched[t - 1], results[t - 1], CUTS[2], CUTS[3])
+            store(t - 1, results[t - 1])
+        best(fetched[TILES - 1], results[TILES - 1])
+        store(TILES - 1, results[TILES - 1])

from contextlib import ExitStack

import concourse.mybir as mybir

K, T, S, V, U, D = 1024, 2048, 512, 512, 1024, 8
FLOPS = 2 * K * V * S

F32 = mybir.dt.float32
BF16 = mybir.dt.bfloat16
I32 = mybir.dt.int32
U32 = mybir.dt.uint32
U16 = mybir.dt.uint16
U8 = mybir.dt.uint8
FP8X4 = mybir.dt.float8_e4m3fn_x4
ALU = mybir.AluOpType
ACT = mybir.ActivationFunctionType
AXIS = mybir.AxisListType

P = 128
PACK = 4
K_PASS = P * PACK
PASSES = K // K_PASS
TILES = V // P
RUN = 2
SCALE_ROWS = 4
SLOPE = 6.0
FADE = 2.4
GROUPS = [(0, P), (P, P), (2 * P, 2 * P)]
HALVES = [(0, S // 2), (S // 2, S)]
WHOLE = [(0, S)]
P_AT = [0, 4, 3, 7]
S_AT = [1, 5, 10, 8]
Y_AT = [9, 2, 6, 5]
CUTS = [0, 64, 96, U // D]


def tile_picked_yplaid_max_p_kernel(tc, x_words, x_scales, hT, offs, code, out):
    nc = tc.nc
    with ExitStack() as ctx:
        keep = ctx.enter_context(tc.tile_pool(name="keep", bufs=1))
        ring = ctx.enter_context(tc.tile_pool(name="ring", bufs=2))
        psum = ctx.enter_context(tc.psum_pool(name="psum", bufs=1))

        offs_sb = keep.tile([P, S // 16], U16, name="offs_sb")
        code_sb = keep.tile([P, U // 16], U16, name="code_sb")
        table = [keep.tile([P, T], U32, name="table%d" % o, align_bytes=64) for o in range(PASSES)]
        table_scales = keep.tile([P, T], U8, name="table_scales", tag="scales_then_words", align_bytes=64)
        picked_scales = keep.tile([P, S], U8, name="picked_scales", align_bytes=64)
        picked = {}
        planes = keep.tile([P, 11 * S], F32, name="planes", align_bytes=64)
        raw, rounded, h_codes, h_scales, banks = {}, {}, {}, {}, {}
        pieces = [HALVES] + [WHOLE] * (TILES - 1)
        for t in range(TILES - 1):
            for first, last in pieces[t]:
                banks[t, first] = psum.tile([P, last - first], F32, name="bank%d_%d" % (t, first), tag="bank%d_%d" % (t, first))

        def p_of(t):
            return planes[:, P_AT[t] * S : (P_AT[t] + 1) * S]

        def s_of(t):
            return planes[:, S_AT[t] * S : (S_AT[t] + 1) * S]

        def y_of(t):
            return planes[:, Y_AT[t] * S : (Y_AT[t] + 1) * S]

        def load_table(o):
            nc.sync.dma_start(
                out=table[o][:].bitcast(I32),
                in_=x_words[o].rearrange("p n r -> p (n r)").bitcast(I32),
            )

        def load_h(g, o):
            c0, w = GROUPS[g]
            raw[g, o] = keep.tile([P, PACK, w], F32, name="raw%d_%d" % (g, o))
            k_rows = hT[o * K_PASS : (o + 1) * K_PASS, c0 : c0 + w]
            nc.sync.dma_start(out=raw[g, o][:], in_=k_rows.rearrange("(p j) t -> p j t", j=PACK))

        def interleave(copy, g, o, dst):
            copy(
                out=dst.rearrange("p (c i j) -> p c j i", i=RUN, j=PACK),
                in_=raw[g, o][:].rearrange("p j (c i) -> p c j i", i=RUN),
            )

        def quantize(g, first, src):
            words = src.shape[1] // PACK
            nc.vector.quantize_mx(
                out=h_codes[g][:, first : first + words].bitcast(FP8X4),
                scales=h_scales[g][:, first : first + words],
                in_=src,
            )

        def pick(o, first, last):
            entries = offs_sb[:, first // 16 : last // 16]
            nc.vector.tensor_copy(picked[o][:, first:last], table[o][:].indirect(entries))

        def product(t, o, first, last):
            g = min(t, len(GROUPS) - 1)
            c0, w = GROUPS[g]
            col = o * w + t * P - c0
            nc.tensor.matmul_mx(
                out=banks[t, first][:],
                lhsT=h_codes[g][:, col : col + P].bitcast(FP8X4),
                lhsT_scale=h_scales[g][:, col : col + P],
                rhs=picked[o][:, first:last].bitcast(FP8X4),
                rhs_scale=picked_scales[SCALE_ROWS * o : P, first:last],
                start=(o == 0),
                stop=(o == PASSES - 1),
            )

        def fade_scaled(t, biases):
            so_far = None
            for (first, last), bias in zip(pieces[t], biases):
                nc.vector.tensor_scalar(
                    out=y_of(t)[:, first:last], in0=banks[t, first][:], scalar1=-FADE, scalar2=so_far,
                    op0=ALU.mult, op1=ALU.min, accum_out=bias,
                )
                so_far = bias
            for first, last in pieces[t]:
                nc.scalar.activation(
                    out=s_of(t)[:, first:last], in_=y_of(t)[:, first:last],
                    func=ACT.Sigmoid, bias=so_far, scale=-SLOPE / FADE,
                )

        def weigh_on_vector(t):
            for first, last in pieces[t]:
                nc.vector.tensor_tensor(
                    out=p_of(t)[:, first:last], in0=banks[t, first][:], in1=s_of(t)[:, first:last], op=ALU.mult
                )

        def fade_plain(t, bias):
            top = keep.tile([P, 1], F32, name="top%d" % t)
            nc.vector.tensor_scalar(
                out=y_of(t), in0=banks[t, 0][:], scalar1=1.0, scalar2=None,
                op0=ALU.mult, op1=ALU.max, accum_out=top[:],
            )
            nc.scalar.mul(bias[:], top[:], -FADE)
            nc.scalar.activation(out=s_of(t), in_=y_of(t), func=ACT.Sigmoid, bias=bias[:], scale=SLOPE)

        def weigh_on_gpsimd(t):
            nc.gpsimd.tensor_tensor(out=p_of(t), in0=y_of(t), in1=s_of(t), op=ALU.mult)

        def fetch(t):
            fetched = ring.tile([P, U // D, D], F32, name="fetched")
            window = planes[:, P_AT[t] * S : (P_AT[t] + 3) * S]
            nc.vector.tensor_copy(fetched[:].rearrange("p v d -> p (v d)"), window.indirect(code_sb[:]))
            return fetched

        def best(fetched, result, first=0, last=U // D):
            nc.vector.tensor_reduce(out=result[:, first:last], in_=fetched[:, first:last, :], axis=AXIS.X, op=ALU.max)

        def store(t, result):
            nc.sync.dma_start(out=out[t * P : (t + 1) * P, :], in_=result)


        nc.gpsimd.memset(table_scales[:].bitcast(I32), 0)
        for q in range(4):
            nc.sync.dma_start(
                out=table_scales[32 * q : 32 * q + SCALE_ROWS * PASSES, :].bitcast(I32),
                in_=x_scales[:, SCALE_ROWS * q : SCALE_ROWS * (q + 1), :].bitcast(I32),
            )
        nc.sync.dma_start(offs_sb[:], offs)
        load_table(0)
        load_h(0, 0)
        load_h(0, 1)
        load_table(1)
        load_h(1, 0)
        load_h(1, 1)
        load_h(2, 0)
        nc.sync.dma_start(code_sb[:], code)
        load_h(2, 1)

        for g, (c0, w) in enumerate(GROUPS):
            h_scales[g] = keep.tile([P, PASSES * w], U8, name="h_scales%d" % g, align_bytes=64)
        for g in range(2):
            rounded[g] = keep.tile([P, PASSES, P * PACK], BF16, name="rounded%d" % g, align_bytes=64)

        picked[0] = keep.tile([P, S], U32, name="picked0", align_bytes=64)
        pick(0, 0, S)
        nc.vector.tensor_copy(picked_scales[:], table_scales[:].indirect(offs_sb[:]))
        for o in range(PASSES):
            interleave(nc.vector.tensor_copy, 0, o, rounded[0][:, o, :])
        h_codes[0] = keep.tile([P, PASSES * P], U32, name="h_codes0", align_bytes=64)
        quantize(0, 0, rounded[0][:].rearrange("p o c -> p (o c)"))
        for first, last in HALVES:
            product(0, 0, first, last)
        picked[1] = keep.tile([P, S], U32, name="picked1", tag="scales_then_words", align_bytes=64)
        for first, last in HALVES:
            pick(1, first, last)
            product(0, 1, first, last)
        half_bias = keep.tile([P, 1], F32, name="half_bias")
        biases = [keep.tile([P, 1], F32, name="bias%d" % t, tag="bias%d" % t, align_bytes=64) for t in range(TILES)]
        h_codes[1] = keep.tile([P, PASSES * P], U32, name="h_codes1", align_bytes=64)
        interleave(nc.vector.tensor_copy, 1, 0, rounded[1][:, 0, :])
        fade_scaled(0, [half_bias[:], biases[0][:]])
        quantize(1, 0, rounded[1][:, 0, :])
        product(1, 0, 0, S)
        interleave(nc.vector.tensor_copy, 1, 1, rounded[1][:, 1, :])
        quantize(1, P, rounded[1][:, 1, :])
        product(1, 1, 0, S)
        weigh_on_vector(0)
        fade_plain(1, biases[1])
        weigh_on_gpsimd(1)

        wide = GROUPS[2][1]
        late = [keep.tile([P, wide * PACK], BF16, name="late%d" % o, tag="bias%d" % o, align_bytes=64) for o in range(PASSES)]
        for o in range(PASSES):
            interleave(nc.scalar.copy, 2, o, late[o][:])
        h_codes[2] = keep.tile([P, PASSES * wide], U32, name="h_codes2", align_bytes=64)
        quantize(2, 0, late[0][:])
        fetched = {0: fetch(0)}
        quantize(2, wide, late[1][:])
        for o in range(PASSES):
            product(2, o, 0, S)
        results = [raw[2, 1][:, t, 0 : U // D] for t in range(TILES)]
        for t in range(1, TILES):
            if t + 1 < TILES:
                best(fetched[t - 1], results[t - 1], CUTS[0], CUTS[1])
                fade_plain(t + 1, biases[t + 1])
                weigh_on_gpsimd(t + 1)
                best(fetched[t - 1], results[t - 1], CUTS[1], CUTS[2])
            else:
                best(fetched[t - 1], results[t - 1], CUTS[0], CUTS[2])
            if t + 2 < TILES:
                banks[t + 2, 0] = psum.tile([P, S], F32, name="bank3_0", tag="bank2_0")
                for o in range(PASSES):
                    product(t + 2, o, 0, S)
            fetched[t] = fetch(t)
            best(fetched[t - 1], results[t - 1], CUTS[2], CUTS[3])
            store(t - 1, results[t - 1])
        best(fetched[TILES - 1], results[TILES - 1])
        store(TILES - 1, results[TILES - 1])
